import numpy as np
import ml_dtypes


def mxq(x, axis, fmt="e4m3"):
    dtype, down = {"e4m3": (ml_dtypes.float8_e4m3fn, 7), "e5m2": (ml_dtypes.float8_e5m2, 14)}[fmt]
    v = np.moveaxis(np.asarray(x, np.float32).astype(ml_dtypes.bfloat16).astype(np.float64), axis, -1)
    blocks = v.reshape(v.shape[:-1] + (-1, 32))
    amax = np.abs(blocks).max(-1, keepdims=True)
    byte = np.maximum(np.where(amax > 0, np.frexp(amax)[1] - 1 + 127, 0) - down, 1)
    scale = np.exp2(byte - 127.0)
    codes = (blocks / scale).astype(np.float32).astype(dtype).astype(np.float64)
    return np.moveaxis((codes * scale).reshape(v.shape), -1, axis)


WIDE = False


def mx_kscale(k):
    if not WIDE:
        return np.ones(k)
    levels = np.array([10, -10, 5, -5, 0])
    if k % 512:
        return np.exp2(np.random.permutation(np.resize(levels, k // 32))).repeat(32)
    a = np.empty((k // 512, 16))
    for p in range(k // 512):
        a[p, :8] = np.random.permutation(np.resize(levels, 8))
        for g in range(8):
            far = levels[np.abs(levels - a[p, g]) >= 10]
            a[p, g + 8] = far[np.random.randint(len(far))]
    return np.exp2(a.ravel()).repeat(32)


def f64(x):
    return np.asarray(x).astype(np.float64)


def striped(idx):
    return np.tile(idx.reshape(-1, 16).T, (8, 1)).astype(np.uint16)


def unstriped(offs):
    return offs[:16].T.reshape(-1).astype(np.int64)


E2M1 = np.array([0.0, 0.5, 1.0, 1.5, 2.0, 3.0, 4.0, 6.0, -0.0, -0.5, -1.0, -1.5, -2.0, -3.0, -4.0, -6.0])


def pack_weight(w, fmt):
    k, n = w.shape
    w = f64(np.asarray(w, np.float32).astype(ml_dtypes.bfloat16)).reshape(k // 32, 32, n)
    amax = np.abs(w).max(1)
    if fmt == "e4m3":
        byte = np.frexp(amax)[1] - 1 + 127 - 7
    else:
        mant, ex = np.frexp(amax / 6.0)
        byte = np.where(mant > 0.5, ex, ex - 1) + 127
    byte = np.clip(np.where(amax > 0, byte, 1), 1, 254)
    scaled = (w * np.exp2(127.0 - byte)[:, None, :]).reshape(k, n).astype(np.float32)
    by_word = np.ascontiguousarray(scaled.reshape(k // 512, 128, 4, n).transpose(0, 1, 3, 2))
    if fmt == "e4m3":
        words = by_word.astype(ml_dtypes.float8_e4m3fn).view(np.uint8)
    else:
        c = by_word.astype(ml_dtypes.float4_e2m1fn).view(np.uint8) & 0xF
        words = (c[..., 0::2] | (c[..., 1::2] << 4)).reshape(k // 512, 128, 2 * n)
    return np.ascontiguousarray(words), np.ascontiguousarray(byte.astype(np.uint8).reshape(k // 512, 16, n))


def unpack_weight(words, scales, fmt):
    g, _, n = scales.shape
    words = np.ascontiguousarray(words).reshape(g, 128, n, -1)
    if fmt == "e4m3":
        vals = words.view(ml_dtypes.float8_e4m3fn).astype(np.float64)
    else:
        nib = np.empty((g, 128, n, 4), np.uint8)
        nib[..., 0::2] = words & 0xF
        nib[..., 1::2] = words >> 4
        vals = E2M1[nib]
    vals = vals * np.repeat(np.exp2(scales.astype(np.float64) - 127.0), 8, axis=1)[..., None]
    return vals.transpose(0, 1, 3, 2).reshape(g * 512, n)


def gelu(v):
    return 0.5 * v * (1.0 + np.tanh(np.sqrt(2.0 / np.pi) * (v + 0.044715 * v**3)))


K, H, N, T, S, T2, P = 1536, 1024, 768, 2048, 512, 1024, 512


def setup_inputs():
    n = np.random.standard_normal
    s = mx_kscale(K)[:, None]
    u = mx_kscale(H)[:, None]
    d = {}
    d["tab_words"], d["tab_scales"] = pack_weight(n((K, T)) * s, "e4m3")
    d["offs"] = striped(np.random.permutation(T)[:S])
    d["w1"] = (n((K, H)) / s * u.T / K ** 0.5).astype(np.float32)
    d["gm"] = np.exp(0.4 * n((H, S))).astype(np.float32)
    d["wgs"] = np.exp(0.3 * n((128, S))).astype(np.float32)
    d["page0"] = (n((H, T2)) * u).astype(np.float32)
    d["offs2"] = striped(np.random.permutation(T2)[:S])
    d["offs3"] = striped(np.random.permutation(T2)[:P])
    d["gain"] = np.exp(0.3 * n(H)).astype(np.float32)
    d["w2"] = (n((H, N)) / u / H ** 0.5).astype(np.float32)
    d["w4_words"], d["w4_scales"] = pack_weight(0.8 * n((H, N)) / u / H ** 0.5, "e2m1")
    d["wgo"] = np.exp(0.3 * n((128, P))).astype(np.float32)
    d["page1"] = n((N, T2)).astype(np.float32)
    d["offs4"] = striped(np.random.permutation(T2)[:P])
    return d


def reference(tab_words, tab_scales, offs, w1, gm, wgs, page0, offs2, offs3, gain, w2, w4_words, w4_scales, wgo, page1, offs4):
    v = unpack_weight(tab_words, tab_scales, "e4m3")[:, unstriped(offs)]
    h = (mxq(f64(w1), 0, "e4m3").T @ v) * f64(gm)
    page = f64(page0).copy()
    page[:, unstriped(offs2)] = np.tile(f64(wgs), (H // 128, 1)) * h
    x = page[:, unstriped(offs3)] * f64(gain)[:, None]
    xq = mxq(x, 0, "e4m3")
    ya = mxq(f64(w2), 0, "e4m3").T @ xq
    yb = unpack_weight(w4_words, w4_scales, "e2m1").T @ xq
    y = ya / (1.0 + np.square(yb))
    out = f64(page1).copy()
    out[:, unstriped(offs4)] = np.tile(f64(wgo), (N // 128, 1)) * y
    return out

@@ -1,0 +1,276 @@
+from contextlib import ExitStack
+
+import concourse.mybir as mybir
+
+K, H, N, T, S, T2, R = 1536, 1024, 768, 2048, 512, 1024, 512
+FLOPS = 2 * K * H * S + 2 * 2 * H * N * R
+
+F32 = mybir.dt.float32
+BF16 = mybir.dt.bfloat16
+I32 = mybir.dt.int32
+U32 = mybir.dt.uint32
+U16 = mybir.dt.uint16
+U8 = mybir.dt.uint8
+FP8X4 = mybir.dt.float8_e4m3fn_x4
+FP4X4 = mybir.dt.float4_e2m1fn_x4
+MULT = mybir.AluOpType.mult
+ACT = mybir.ActivationFunctionType
+
+P = 128
+PACK = 4
+KP = P * PACK
+
+
+def tile_list_hide_cutter_page_kernel(tc, tab_words, tab_scales, offs, w1, gm, wgs, page0, offs2, offs3, gain, w2, w4_words, w4_scales, wgo, page1, offs4, out):
+    nc = tc.nc
+    ka = K // KP
+    hb = H // KP
+    nm = N // P
+    with ExitStack() as ctx:
+        lists = ctx.enter_context(tc.tile_pool(name="lists", bufs=1))
+        keep = ctx.enter_context(tc.tile_pool(name="keep", bufs=1))
+        ring = ctx.enter_context(tc.tile_pool(name="ring", bufs=3))
+        psum = ctx.enter_context(tc.psum_pool(name="psum", bufs=8))
+
+        def load_list(src, name):
+            t = lists.tile([P, src.shape[1]], U16, name=name)
+            nc.sync.dma_start(t[:], src)
+            return t
+
+        idx = load_list(offs, "idx")
+        tab_sc = keep.tile([P, T], U8, name="tab_sc")
+        nc.gpsimd.memset(tab_sc[:].bitcast(I32), 0)
+        w4_sc = keep.tile([P, hb * N], U8, name="w4_sc", align_bytes=64)
+        nc.gpsimd.memset(w4_sc[:].bitcast(I32), 0)
+        seed = keep.tile([P, 1], F32, name="seed")
+        nc.gpsimd.memset(seed[:], 1.0)
+        warm = keep.tile([P, 1], F32, name="warm")
+        nc.scalar.activation(warm[:], seed[:], ACT.Abs_reciprocal_sqrt)
+        one = keep.tile([P, 1], F32, name="one")
+        nc.scalar.activation(one[:], warm[:], ACT.Copy, scale=0.0, bias=1.0)
+
+        def load_rows(w, a, c0, c1, tag="raw", bufs=3):
+            raw = ring.tile([P, PACK, c1 - c0], F32, name="raw", tag=tag, bufs=bufs)
+            nc.sync.dma_start(raw[:], w[a * KP : (a + 1) * KP, c0:c1].rearrange("(p j) c -> p j c", j=PACK))
+            return raw
+
+        def quantize(grouped, codes, scales):
+            nc.vector.quantize_mx(out=codes.bitcast(FP8X4), scales=scales, in_=grouped)
+
+        def w1_chunk(raw, a, b):
+            grouped = ring.tile([P, PACK * KP], BF16, name="grouped", tag="grouped", align_bytes=64)
+            nc.scalar.copy(
+                grouped[:].rearrange("p (t m j) -> p m t j", t=PACK, j=PACK),
+                raw[:].rearrange("p j (m t) -> p m t j", t=PACK),
+            )
+            codes = keep.tile([P, KP], U32, name="w1c%d%d" % (a, b), align_bytes=64)
+            scales = keep.tile([P, KP], U8, name="w1s%d%d" % (a, b), align_bytes=64)
+            quantize(grouped[:], codes[:], scales[:])
+            return codes, scales
+
+        w1q = {}
+        for a in range(ka):
+            w1q[a, 0] = w1_chunk(load_rows(w1, a, 0, KP), a, 0)
+            if a == 1:
+                for q in range(4):
+                    nc.sync.dma_start(tab_sc[32 * q : 32 * q + 4 * ka, :].bitcast(I32), tab_scales[:, 4 * q : 4 * q + 4, :].bitcast(I32))
+
+        v_sc = keep.tile([P, S], U8, name="v_sc", align_bytes=64)
+        nc.vector.tensor_copy(v_sc[:], tab_sc[:].indirect(idx[:]))
+        v_codes = []
+        for a in range(ka):
+            tab = ring.tile([P, T], I32, name="tab", tag="tab")
+            nc.sync.dma_start(tab[:], tab_words[a].rearrange("p t i -> p (t i)").bitcast(I32))
+            vc = keep.tile([P, S], U32, name="vc%d" % a, align_bytes=64)
+            nc.vector.tensor_copy(vc[:], tab[:].bitcast(U32).indirect(idx[:]))
+            v_codes.append(vc)
+
+        def stage1(b):
+            banks = [psum.tile([P, S], F32, name="acc", tag="acc") for t in range(PACK)]
+            for a in range(ka):
+                codes, scales = w1q[a, b]
+                for t in range(PACK):
+                    cols = slice(t * P, (t + 1) * P)
+                    nc.tensor.matmul_mx(
+                        out=banks[t][:], lhsT=codes[:, cols].bitcast(FP8X4), lhsT_scale=scales[:, cols],
+                        rhs=v_codes[a][:].bitcast(FP8X4), rhs_scale=v_sc[4 * a : P, :],
+                        start=(a == 0), stop=(a == ka - 1),
+                    )
+            return banks
+
+        gm_rows = gm.rearrange("(b p t) j -> b t p j", p=P, t=PACK)
+        page0_rows = page0.rearrange("(b p t) j -> b t p j", p=P, t=PACK)
+        wgs_rows = wgs.rearrange("(q t) j -> q t j", t=PACK)
+
+        def load_gm(i):
+            g = ring.tile([P, S], F32, name="gm_sb", tag="gm_sb", bufs=4)
+            nc.sync.dma_start(g[:], gm_rows[i // PACK, i % PACK])
+            return g
+
+        def load_page0(i):
+            pg = keep.tile([P, T2], F32, name="page0_%d" % i)
+            nc.sync.dma_start(pg[:], page0_rows[i // PACK, i % PACK])
+            return pg
+
+        h_banks = stage1(0)
+        gms = [load_gm(0)]
+        wgs_sb = keep.tile([P, PACK, S], F32, name="wgs_sb", tag="late", align_bytes=64)
+        for q in range(4):
+            nc.sync.dma_start(wgs_sb[32 * q : 32 * q + 32, 0, :], wgs_rows[:, 0, :])
+        idx2 = load_list(offs2, "idx2")
+        idx3 = load_list(offs3, "idx3")
+        pages = [load_page0(0)]
+        gms.append(load_gm(1))
+        for q in range(4):
+            nc.sync.dma_start(wgs_sb[32 * q : 32 * q + 32, 1:PACK, :], wgs_rows[:, 1:PACK, :])
+        pages.append(load_page0(1))
+        gms.append(load_gm(2))
+        raws = [load_rows(w1, 0, KP, 2 * KP)]
+        pages.append(load_page0(2))
+        gms.append(load_gm(3))
+        raws.append(load_rows(w1, 1, KP, 2 * KP))
+        raws.append(load_rows(w1, 2, KP, 2 * KP, "raw_last", 1))
+        gain_sb = keep.tile([P, hb * PACK], F32, name="gain_sb")
+        nc.sync.dma_start(gain_sb[:].rearrange("p (b t) -> p b t", b=hb), gain.rearrange("(b p t) -> p b t", b=hb, t=PACK))
+        pages.append(load_page0(3))
+        gms.append(load_gm(4))
+        pages.append(load_page0(4))
+        gms.append(load_gm(5))
+        w2_cuts = ((0, KP), (KP, N))
+        w2_raw = [[load_rows(w2, 0, c0, c1, "tab") for c0, c1 in w2_cuts]]
+        pages.append(load_page0(5))
+        gms.append(load_gm(6))
+        w2_raw.append([load_rows(w2, 1, 0, KP, "tab"), load_rows(w2, 1, KP, N)])
+        pages.append(load_page0(6))
+        gms.append(load_gm(7))
+        pages.append(load_page0(7))
+        for q in range(4):
+            nc.sync.dma_start(
+                w4_sc[32 * q : 32 * q + 4, :].bitcast(I32).rearrange("r (a c) -> r a c", a=hb),
+                w4_scales[:, 4 * q : 4 * q + 4, :].bitcast(I32).rearrange("a r c -> r a c"),
+            )
+        w4_sb = keep.tile([P, hb * 2 * N], U8, name="w4_sb", align_bytes=64)
+        nc.sync.dma_start(w4_sb[:].bitcast(I32).rearrange("p (a c) -> p a c", a=hb), w4_words.bitcast(I32).rearrange("a p c -> p a c"))
+        wgo_sb = keep.tile([P, R], F32, name="wgo_sb")
+        nc.sync.dma_start(wgo_sb[:], wgo)
+        idx4 = load_list(offs4, "idx4")
+        cutter = []
+        for m in range(nm):
+            pg = keep.tile([P, T2], F32, name="page1_%d" % m)
+            nc.sync.dma_start(pg[:], page1[m * P : (m + 1) * P, :])
+            cutter.append(pg)
+
+        HALF = R // 2
+        LC = HALF // 16
+        hs = {}
+
+        def make_h(i):
+            hs[i] = ring.tile([P, S], F32, name="h", tag="h")
+            nc.vector.tensor_tensor(hs[i][:], h_banks[i][:], gms[i][:], MULT)
+
+        def put_h(i):
+            nc.vector.tensor_tensor(pages[i][:].indirect(idx2[:]), hs[i][:], wgs_sb[:, i % PACK, :], MULT)
+
+        def pick(i, c0, c1, dst):
+            nc.vector.tensor_copy(dst, pages[i][:].indirect(idx3[:, c0 // 16 : c1 // 16]))
+
+        def scale_rows(i, src, rows):
+            nc.scalar.activation(rows[:, i % PACK, :], src, ACT.Copy, scale=gain_sb[:, i : i + 1])
+
+        xq = [
+            (keep.tile([P, R], U32, name="xc%d" % b, align_bytes=64), keep.tile([P, R], U8, name="xs%d" % b, align_bytes=64))
+            for b in range(hb)
+        ]
+
+        def quantize_x(rows, b, c0, c1, tag="grouped", bufs=3):
+            grouped = ring.tile([P, PACK * (c1 - c0)], BF16, name="grouped", tag=tag, bufs=bufs, align_bytes=64)
+            nc.scalar.copy(
+                grouped[:].rearrange("p (c i t) -> p c t i", i=4, t=PACK),
+                rows[:].rearrange("p t (c i) -> p c t i", i=4),
+            )
+            quantize(grouped[:], xq[b][0][:, c0:c1], xq[b][1][:, c0:c1])
+
+        w2_grouped = keep.tile([P, hb * N * PACK], BF16, name="w2_grouped", align_bytes=64)
+
+        def w2_cast(a):
+            for (c0, c1), raw in zip(w2_cuts, w2_raw[a]):
+                nc.scalar.copy(
+                    w2_grouped[:].rearrange("p (m a c i j) -> p a m c j i", a=hb, c=P // 4, i=4, j=PACK)[:, a, c0 // P : c1 // P],
+                    raw[:].rearrange("p j (m c i) -> p m c j i", c=P // 4, i=4),
+                )
+
+        picked = keep.tile([P, PACK, R], F32, name="picked")
+        make_h(0)
+        for i in range(PACK):
+            put_h(i)
+            if i < PACK - 1:
+                make_h(i + 1)
+                w1q[i, 1] = w1_chunk(raws[i], i, 1)
+            pick(i, 0, R, picked[:, i, :])
+        h_banks.extend(stage1(1))
+        make_h(PACK)
+        pass
+        rows = ring.tile([P, PACK, R], BF16, name="rows", tag="raw_last", bufs=1)
+        for i in range(PACK):
+            scale_rows(i, picked[:, i, :], rows)
+        quantize_x(rows, 0, 0, R)
+        picked = keep.tile([P, PACK, HALF], F32, name="picked_a")
+        rows = keep.tile([P, PACK, HALF], BF16, name="rows_a")
+        for i in range(PACK, 2 * PACK):
+            put_h(i)
+            if i < 2 * PACK - 1:
+                make_h(i + 1)
+            pick(i, 0, HALF, picked[:, i - PACK, :])
+            scale_rows(i, picked[:, i - PACK, :], rows)
+            if i - PACK < hb:
+                w2_cast(i - PACK)
+        quantize_x(rows, 1, 0, HALF, "late_codes", 1)
+        pass
+        w2_codes = ring.tile([P, hb * N], U32, name="w2_codes", tag="late_codes", bufs=1, align_bytes=64)
+        w2_scales = keep.tile([P, hb * N], U8, name="w2_scales", align_bytes=64)
+        picked = keep.tile([P, PACK, HALF], F32, name="picked_b", tag="late", align_bytes=64)
+        rows = keep.tile([P, PACK, HALF], BF16, name="rows_b")
+        for i in range(PACK, 2 * PACK):
+            pick(i, HALF, R, picked[:, i - PACK, :])
+            scale_rows(i, picked[:, i - PACK, :], rows)
+        for c0, c1 in ((0, 1024), (1024, hb * N)):
+            quantize(w2_grouped[:, c0 * PACK : c1 * PACK], w2_codes[:, c0:c1], w2_scales[:, c0:c1])
+        quantize_x(rows, 1, HALF, R)
+
+        def unit(u, m0, cnt):
+            yb = psum.tile([P, cnt, HALF], F32, name="acc", tag="acc")
+            ya = psum.tile([P, cnt, HALF], F32, name="acc", tag="acc")
+            for d in range(cnt):
+                m = m0 + d
+                for c0 in range(0, HALF, P):
+                    for a in range(hb):
+                        nc.tensor.matmul_mx(
+                            out=yb[:, d, c0 : c0 + P], lhsT=w4_sb[:, a * 2 * N + 2 * m * P : a * 2 * N + 2 * (m + 1) * P].bitcast(FP4X4),
+                            lhsT_scale=w4_sc[:, a * N + m * P : a * N + (m + 1) * P],
+                            rhs=xq[a][0][:, u * HALF + c0 : u * HALF + c0 + P].bitcast(FP8X4), rhs_scale=xq[a][1][:, u * HALF + c0 : u * HALF + c0 + P], start=(a == 0), stop=(a == hb - 1),
+                        )
+            for d in range(cnt):
+                m = m0 + d
+                for a in range(hb):
+                    nc.tensor.matmul_mx(
+                        out=ya[:, d, :], lhsT=w2_codes[:, (m * hb + a) * P : (m * hb + a + 1) * P].bitcast(FP8X4), lhsT_scale=w2_scales[:, (m * hb + a) * P : (m * hb + a + 1) * P],
+                        rhs=xq[a][0][:, u * HALF : (u + 1) * HALF].bitcast(FP8X4), rhs_scale=xq[a][1][:, u * HALF : (u + 1) * HALF], start=(a == 0), stop=(a == hb - 1),
+                    )
+            sq = ring.tile([P, cnt * HALF], F32, name="sq", tag="sq", bufs=1)
+            nc.scalar.activation(sq[:], yb[:].rearrange("p d c -> p (d c)"), ACT.Square)
+            rs = ring.tile([P, cnt * HALF], F32, name="rs", tag="rs", bufs=1)
+            nc.scalar.activation(rs[:], sq[:], ACT.Abs_reciprocal_sqrt, bias=one[:])
+            damp = ring.tile([P, cnt * HALF], F32, name="damp", tag="damp", bufs=2)
+            nc.scalar.activation(damp[:], rs[:], ACT.Square)
+            y = ring.tile([P, cnt * HALF], F32, name="y", tag="h")
+            nc.vector.tensor_tensor(y[:], ya[:].rearrange("p d c -> p (d c)"), damp[:], MULT)
+            for d in range(cnt):
+                m = m0 + d
+                nc.vector.tensor_tensor(
+                    cutter[m][:].indirect(idx4[:, u * LC : (u + 1) * LC]), y[:, d * HALF : (d + 1) * HALF], wgo_sb[:, u * HALF : (u + 1) * HALF], MULT
+                )
+                if u == 1:
+                    nc.sync.dma_start(out[m * P : (m + 1) * P, :], cutter[m][:])
+
+        for u, m0, cnt in ((0, 0, 1), (0, 1, 1), (0, 2, 2), (1, 0, 2), (0, 4, 2), (1, 2, 2), (1, 4, 2)):
+            unit(u, m0, cnt)

@@ -30,7 +30,14 @@ def tile_list_hide_cutter_page_kernel(tc, tab_words, tab_scales, offs, w1, gm, w
         lists = ctx.enter_context(tc.tile_pool(name="lists", bufs=1))
         keep = ctx.enter_context(tc.tile_pool(name="keep", bufs=1))
         ring = ctx.enter_context(tc.tile_pool(name="ring", bufs=3))
-        psum = ctx.enter_context(tc.psum_pool(name="psum", bufs=8))
+        psum = ctx.enter_context(tc.psum_pool(name="psum", bufs=1))
+
+        turns = {}
+
+        def turn(pool, shape, dtype, tag, slots, align=None):
+            k = turns.get(tag, 0)
+            turns[tag] = k + 1
+            return pool.tile(shape, dtype, name=tag, tag="%s%d" % (tag, k % slots), bufs=1, align_bytes=align)
 
         def load_list(src, name):
             t = lists.tile([P, src.shape[1]], U16, name=name)
@@ -50,7 +57,7 @@ def tile_list_hide_cutter_page_kernel(tc, tab_words, tab_scales, offs, w1, gm, w
         nc.scalar.activation(one[:], warm[:], ACT.Copy, scale=0.0, bias=1.0)
 
         def load_rows(w, a, c0, c1, tag="raw", bufs=3):
-            raw = ring.tile([P, PACK, c1 - c0], F32, name="raw", tag=tag, bufs=bufs)
+            raw = turn(ring, [P, PACK, c1 - c0], F32, tag, bufs)
             nc.sync.dma_start(raw[:], w[a * KP : (a + 1) * KP, c0:c1].rearrange("(p j) c -> p j c", j=PACK))
             return raw
 
@@ -58,7 +65,7 @@ def tile_list_hide_cutter_page_kernel(tc, tab_words, tab_scales, offs, w1, gm, w
             nc.vector.quantize_mx(out=codes.bitcast(FP8X4), scales=scales, in_=grouped)
 
         def w1_chunk(raw, a, b):
-            grouped = ring.tile([P, PACK * KP], BF16, name="grouped", tag="grouped", align_bytes=64)
+            grouped = turn(ring, [P, PACK * KP], BF16, "grouped", 3, 64)
             nc.scalar.copy(
                 grouped[:].rearrange("p (t m j) -> p m t j", t=PACK, j=PACK),
                 raw[:].rearrange("p j (m t) -> p m t j", t=PACK),
@@ -79,14 +86,14 @@ def tile_list_hide_cutter_page_kernel(tc, tab_words, tab_scales, offs, w1, gm, w
         nc.vector.tensor_copy(v_sc[:], tab_sc[:].indirect(idx[:]))
         v_codes = []
         for a in range(ka):
-            tab = ring.tile([P, T], I32, name="tab", tag="tab")
+            tab = turn(ring, [P, T], I32, "tab", 3)
             nc.sync.dma_start(tab[:], tab_words[a].rearrange("p t i -> p (t i)").bitcast(I32))
             vc = keep.tile([P, S], U32, name="vc%d" % a, align_bytes=64)
             nc.vector.tensor_copy(vc[:], tab[:].bitcast(U32).indirect(idx[:]))
             v_codes.append(vc)
 
         def stage1(b):
-            banks = [psum.tile([P, S], F32, name="acc", tag="acc") for t in range(PACK)]
+            banks = [turn(psum, [P, S], F32, "acc", 8) for t in range(PACK)]
             for a in range(ka):
                 codes, scales = w1q[a, b]
                 for t in range(PACK):
@@ -103,7 +110,7 @@ def tile_list_hide_cutter_page_kernel(tc, tab_words, tab_scales, offs, w1, gm, w
         wgs_rows = wgs.rearrange("(q t) j -> q t j", t=PACK)
 
         def load_gm(i):
-            g = ring.tile([P, S], F32, name="gm_sb", tag="gm_sb", bufs=4)
+            g = turn(ring, [P, S], F32, "gm_sb", 4)
             nc.sync.dma_start(g[:], gm_rows[i // PACK, i % PACK])
             return g
 
@@ -165,11 +172,17 @@ def tile_list_hide_cutter_page_kernel(tc, tab_words, tab_scales, offs, w1, gm, w
         hs = {}
 
         def make_h(i):
-            hs[i] = ring.tile([P, S], F32, name="h", tag="h")
-            nc.vector.tensor_tensor(hs[i][:], h_banks[i][:], gms[i][:], MULT)
+            last = i == 2 * PACK - 1
+            hs[i] = turn(ring, [P, S], F32, "h_last", 1) if last else turn(ring, [P, S], F32, "h", 5)
+            nc.gpsimd.tensor_tensor(gms[i][:], gms[i][:], wgs_sb[:, i % PACK, :], MULT)
+            if i % PACK == 0:
+                nc.vector.tensor_tensor(hs[i][:], h_banks[i][:], gms[i][:], MULT)
+            else:
+                nc.scalar.copy(hs[i][:], h_banks[i][:])
+                nc.gpsimd.tensor_tensor(hs[i][:], hs[i][:], gms[i][:], MULT)
 
         def put_h(i):
-            nc.vector.tensor_tensor(pages[i][:].indirect(idx2[:]), hs[i][:], wgs_sb[:, i % PACK, :], MULT)
+            nc.vector.tensor_copy(pages[i][:].indirect(idx2[:]), hs[i][:])
 
         def pick(i, c0, c1, dst):
             nc.vector.tensor_copy(dst, pages[i][:].indirect(idx3[:, c0 // 16 : c1 // 16]))
@@ -183,7 +196,7 @@ def tile_list_hide_cutter_page_kernel(tc, tab_words, tab_scales, offs, w1, gm, w
         ]
 
         def quantize_x(rows, b, c0, c1, tag="grouped", bufs=3):
-            grouped = ring.tile([P, PACK * (c1 - c0)], BF16, name="grouped", tag=tag, bufs=bufs, align_bytes=64)
+            grouped = turn(ring, [P, PACK * (c1 - c0)], BF16, tag, bufs, 64)
             nc.scalar.copy(
                 grouped[:].rearrange("p (c i t) -> p c t i", i=4, t=PACK),
                 rows[:].rearrange("p t (c i) -> p c t i", i=4),
@@ -208,9 +221,10 @@ def tile_list_hide_cutter_page_kernel(tc, tab_words, tab_scales, offs, w1, gm, w
                 w1q[i, 1] = w1_chunk(raws[i], i, 1)
             pick(i, 0, R, picked[:, i, :])
         h_banks.extend(stage1(1))
-        make_h(PACK)
+        for i in range(PACK, 2 * PACK):
+            make_h(i)
         pass
-        rows = ring.tile([P, PACK, R], BF16, name="rows", tag="raw_last", bufs=1)
+        rows = turn(ring, [P, PACK, R], BF16, "raw_last", 1)
         for i in range(PACK):
             scale_rows(i, picked[:, i, :], rows)
         quantize_x(rows, 0, 0, R)
@@ -218,28 +232,24 @@ def tile_list_hide_cutter_page_kernel(tc, tab_words, tab_scales, offs, w1, gm, w
         rows = keep.tile([P, PACK, HALF], BF16, name="rows_a")
         for i in range(PACK, 2 * PACK):
             put_h(i)
-            if i < 2 * PACK - 1:
-                make_h(i + 1)
             pick(i, 0, HALF, picked[:, i - PACK, :])
             scale_rows(i, picked[:, i - PACK, :], rows)
             if i - PACK < hb:
                 w2_cast(i - PACK)
         quantize_x(rows, 1, 0, HALF, "late_codes", 1)
         pass
-        w2_codes = ring.tile([P, hb * N], U32, name="w2_codes", tag="late_codes", bufs=1, align_bytes=64)
+        w2_codes = turn(ring, [P, hb * N], U32, "late_codes", 1, 64)
         w2_scales = keep.tile([P, hb * N], U8, name="w2_scales", align_bytes=64)
-        picked = keep.tile([P, PACK, HALF], F32, name="picked_b", tag="late", align_bytes=64)
+        picked = turn(ring, [P, PACK, HALF], F32, "h_last", 1)
         rows = keep.tile([P, PACK, HALF], BF16, name="rows_b")
         for i in range(PACK, 2 * PACK):
             pick(i, HALF, R, picked[:, i - PACK, :])
-            scale_rows(i, picked[:, i - PACK, :], rows)
         for c0, c1 in ((0, 1024), (1024, hb * N)):
             quantize(w2_grouped[:, c0 * PACK : c1 * PACK], w2_codes[:, c0:c1], w2_scales[:, c0:c1])
-        quantize_x(rows, 1, HALF, R)
 
         def unit(u, m0, cnt):
-            yb = psum.tile([P, cnt, HALF], F32, name="acc", tag="acc")
-            ya = psum.tile([P, cnt, HALF], F32, name="acc", tag="acc")
+            yb = turn(psum, [P, cnt, HALF], F32, "acc", 8)
+            ya = turn(psum, [P, cnt, HALF], F32, "acc", 8)
             for d in range(cnt):
                 m = m0 + d
                 for c0 in range(0, HALF, P):
@@ -256,21 +266,27 @@ def tile_list_hide_cutter_page_kernel(tc, tab_words, tab_scales, offs, w1, gm, w
                         out=ya[:, d, :], lhsT=w2_codes[:, (m * hb + a) * P : (m * hb + a + 1) * P].bitcast(FP8X4), lhsT_scale=w2_scales[:, (m * hb + a) * P : (m * hb + a + 1) * P],
                         rhs=xq[a][0][:, u * HALF : (u + 1) * HALF].bitcast(FP8X4), rhs_scale=xq[a][1][:, u * HALF : (u + 1) * HALF], start=(a == 0), stop=(a == hb - 1),
                     )
+            y = turn(ring, [P, cnt * HALF], F32, "raw" if u == 0 else "tab", 3)
+            nc.scalar.copy(y[:], ya[:].rearrange("p d c -> p (d c)"))
+            y3 = y[:].rearrange("p (d c) -> p d c", d=cnt)
+            nc.gpsimd.tensor_tensor(y3, y3, wgo_sb[:, u * HALF : (u + 1) * HALF].unsqueeze(1).to_broadcast([P, cnt, HALF]), MULT)
             sq = ring.tile([P, cnt * HALF], F32, name="sq", tag="sq", bufs=1)
             nc.scalar.activation(sq[:], yb[:].rearrange("p d c -> p (d c)"), ACT.Square)
             rs = ring.tile([P, cnt * HALF], F32, name="rs", tag="rs", bufs=1)
             nc.scalar.activation(rs[:], sq[:], ACT.Abs_reciprocal_sqrt, bias=one[:])
-            damp = ring.tile([P, cnt * HALF], F32, name="damp", tag="damp", bufs=2)
+            damp = turn(ring, [P, cnt * HALF], F32, "gm_sb", 4)
             nc.scalar.activation(damp[:], rs[:], ACT.Square)
-            y = ring.tile([P, cnt * HALF], F32, name="y", tag="h")
-            nc.vector.tensor_tensor(y[:], ya[:].rearrange("p d c -> p (d c)"), damp[:], MULT)
+            nc.gpsimd.tensor_tensor(y[:], y[:], damp[:], MULT)
             for d in range(cnt):
                 m = m0 + d
-                nc.vector.tensor_tensor(
-                    cutter[m][:].indirect(idx4[:, u * LC : (u + 1) * LC]), y[:, d * HALF : (d + 1) * HALF], wgo_sb[:, u * HALF : (u + 1) * HALF], MULT
-                )
+                nc.vector.tensor_copy(cutter[m][:].indirect(idx4[:, u * LC : (u + 1) * LC]), y[:, d * HALF : (d + 1) * HALF])
                 if u == 1:
                     nc.sync.dma_start(out[m * P : (m + 1) * P, :], cutter[m][:])
 
-        for u, m0, cnt in ((0, 0, 1), (0, 1, 1), (0, 2, 2), (1, 0, 2), (0, 4, 2), (1, 2, 2), (1, 4, 2)):
+        unit(0, 0, 1)
+        unit(0, 1, 1)
+        for i in range(PACK, 2 * PACK):
+            scale_rows(i, picked[:, i - PACK, :], rows)
+        quantize_x(rows, 1, HALF, R)
+        for u, m0, cnt in ((0, 2, 2), (0, 4, 2), (1, 0, 2), (1, 2, 2), (1, 4, 2)):
             unit(u, m0, cnt)

@@ -66,7 +66,8 @@ def tile_list_hide_cutter_page_kernel(tc, tab_words, tab_scales, offs, w1, gm, w
 
         def w1_chunk(raw, a, b):
             grouped = turn(ring, [P, PACK * KP], BF16, "grouped", 3, 64)
-            nc.scalar.copy(
+            cast = nc.vector.tensor_copy if (a, b) == (1, 0) else nc.scalar.copy
+            cast(
                 grouped[:].rearrange("p (t m j) -> p m t j", t=PACK, j=PACK),
                 raw[:].rearrange("p j (m t) -> p m t j", t=PACK),
             )
@@ -76,21 +77,25 @@ def tile_list_hide_cutter_page_kernel(tc, tab_words, tab_scales, offs, w1, gm, w
             return codes, scales
 
         w1q = {}
-        for a in range(ka):
-            w1q[a, 0] = w1_chunk(load_rows(w1, a, 0, KP), a, 0)
-            if a == 1:
-                for q in range(4):
-                    nc.sync.dma_start(tab_sc[32 * q : 32 * q + 4 * ka, :].bitcast(I32), tab_scales[:, 4 * q : 4 * q + 4, :].bitcast(I32))
-
-        v_sc = keep.tile([P, S], U8, name="v_sc", align_bytes=64)
-        nc.vector.tensor_copy(v_sc[:], tab_sc[:].indirect(idx[:]))
         v_codes = []
-        for a in range(ka):
+
+        def gather_pass(a):
             tab = turn(ring, [P, T], I32, "tab", 3)
             nc.sync.dma_start(tab[:], tab_words[a].rearrange("p t i -> p (t i)").bitcast(I32))
             vc = keep.tile([P, S], U32, name="vc%d" % a, align_bytes=64)
             nc.vector.tensor_copy(vc[:], tab[:].bitcast(U32).indirect(idx[:]))
             v_codes.append(vc)
+
+        for a in range(2):
+            w1q[a, 0] = w1_chunk(load_rows(w1, a, 0, KP), a, 0)
+        for q in range(4):
+            nc.sync.dma_start(tab_sc[32 * q : 32 * q + 4 * ka, :].bitcast(I32), tab_scales[:, 4 * q : 4 * q + 4, :].bitcast(I32))
+        v_sc = keep.tile([P, S], U8, name="v_sc", align_bytes=64)
+        nc.vector.tensor_copy(v_sc[:], tab_sc[:].indirect(idx[:]))
+        gather_pass(0)
+        w1q[2, 0] = w1_chunk(load_rows(w1, 2, 0, KP), 2, 0)
+        gather_pass(1)
+        gather_pass(2)
 
         def stage1(b):
             banks = [turn(psum, [P, S], F32, "acc", 8) for t in range(PACK)]
@@ -122,13 +127,13 @@ def tile_list_hide_cutter_page_kernel(tc, tab_words, tab_scales, offs, w1, gm, w
         h_banks = stage1(0)
         gms = [load_gm(0)]
         wgs_sb = keep.tile([P, PACK, S], F32, name="wgs_sb", tag="late", align_bytes=64)
-        for q in range(4):
+        for q in (0, 2, 1, 3):
             nc.sync.dma_start(wgs_sb[32 * q : 32 * q + 32, 0, :], wgs_rows[:, 0, :])
         idx2 = load_list(offs2, "idx2")
         idx3 = load_list(offs3, "idx3")
         pages = [load_page0(0)]
         gms.append(load_gm(1))
-        for q in range(4):
+        for q in (0, 2, 1, 3):
             nc.sync.dma_start(wgs_sb[32 * q : 32 * q + 32, 1:PACK, :], wgs_rows[:, 1:PACK, :])
         pages.append(load_page0(1))
         gms.append(load_gm(2))
@@ -168,21 +173,14 @@ def tile_list_hide_cutter_page_kernel(tc, tab_words, tab_scales, offs, w1, gm, w
             cutter.append(pg)
 
         HALF = R // 2
-        LC = HALF // 16
         hs = {}
 
         def make_h(i):
-            last = i == 2 * PACK - 1
-            hs[i] = turn(ring, [P, S], F32, "h_last", 1) if last else turn(ring, [P, S], F32, "h", 5)
-            nc.gpsimd.tensor_tensor(gms[i][:], gms[i][:], wgs_sb[:, i % PACK, :], MULT)
-            if i % PACK == 0:
-                nc.vector.tensor_tensor(hs[i][:], h_banks[i][:], gms[i][:], MULT)
-            else:
-                nc.scalar.copy(hs[i][:], h_banks[i][:])
-                nc.gpsimd.tensor_tensor(hs[i][:], hs[i][:], gms[i][:], MULT)
+            hs[i] = turn(ring, [P, S], F32, "h", 3)
+            nc.vector.tensor_tensor(hs[i][:], h_banks[i][:], gms[i][:], MULT)
 
         def put_h(i):
-            nc.vector.tensor_copy(pages[i][:].indirect(idx2[:]), hs[i][:])
+            nc.vector.tensor_tensor(pages[i][:].indirect(idx2[:]), hs[i][:], wgs_sb[:, i % PACK, :], MULT)
 
         def pick(i, c0, c1, dst):
             nc.vector.tensor_copy(dst, pages[i][:].indirect(idx3[:, c0 // 16 : c1 // 16]))
@@ -221,8 +219,7 @@ def tile_list_hide_cutter_page_kernel(tc, tab_words, tab_scales, offs, w1, gm, w
                 w1q[i, 1] = w1_chunk(raws[i], i, 1)
             pick(i, 0, R, picked[:, i, :])
         h_banks.extend(stage1(1))
-        for i in range(PACK, 2 * PACK):
-            make_h(i)
+        make_h(PACK)
         pass
         rows = turn(ring, [P, PACK, R], BF16, "raw_last", 1)
         for i in range(PACK):
@@ -232,6 +229,8 @@ def tile_list_hide_cutter_page_kernel(tc, tab_words, tab_scales, offs, w1, gm, w
         rows = keep.tile([P, PACK, HALF], BF16, name="rows_a")
         for i in range(PACK, 2 * PACK):
             put_h(i)
+            if i < 2 * PACK - 1:
+                make_h(i + 1)
             pick(i, 0, HALF, picked[:, i - PACK, :])
             scale_rows(i, picked[:, i - PACK, :], rows)
             if i - PACK < hb:
@@ -240,53 +239,56 @@ def tile_list_hide_cutter_page_kernel(tc, tab_words, tab_scales, offs, w1, gm, w
         pass
         w2_codes = turn(ring, [P, hb * N], U32, "late_codes", 1, 64)
         w2_scales = keep.tile([P, hb * N], U8, name="w2_scales", align_bytes=64)
-        picked = turn(ring, [P, PACK, HALF], F32, "h_last", 1)
+        picked = keep.tile([P, PACK, HALF], F32, name="picked_b", tag="late", align_bytes=64)
         rows = keep.tile([P, PACK, HALF], BF16, name="rows_b")
         for i in range(PACK, 2 * PACK):
             pick(i, HALF, R, picked[:, i - PACK, :])
         for c0, c1 in ((0, 1024), (1024, hb * N)):
             quantize(w2_grouped[:, c0 * PACK : c1 * PACK], w2_codes[:, c0:c1], w2_scales[:, c0:c1])
 
-        def unit(u, m0, cnt):
-            yb = turn(psum, [P, cnt, HALF], F32, "acc", 8)
-            ya = turn(psum, [P, cnt, HALF], F32, "acc", 8)
+        def unit(m0, cnt, j0, j1):
+            width = j1 - j0
+            yb = turn(psum, [P, cnt, width], F32, "acc", 8)
+            ya = turn(psum, [P, cnt, width], F32, "acc", 8)
+            step = R if width == R else P
             for d in range(cnt):
                 m = m0 + d
-                for c0 in range(0, HALF, P):
+                for c0 in range(0, width, step):
+                    cols = slice(j0 + c0, j0 + c0 + step)
                     for a in range(hb):
                         nc.tensor.matmul_mx(
-                            out=yb[:, d, c0 : c0 + P], lhsT=w4_sb[:, a * 2 * N + 2 * m * P : a * 2 * N + 2 * (m + 1) * P].bitcast(FP4X4),
+                            out=yb[:, d, c0 : c0 + step], lhsT=w4_sb[:, a * 2 * N + 2 * m * P : a * 2 * N + 2 * (m + 1) * P].bitcast(FP4X4),
                             lhsT_scale=w4_sc[:, a * N + m * P : a * N + (m + 1) * P],
-                            rhs=xq[a][0][:, u * HALF + c0 : u * HALF + c0 + P].bitcast(FP8X4), rhs_scale=xq[a][1][:, u * HALF + c0 : u * HALF + c0 + P], start=(a == 0), stop=(a == hb - 1),
+                            rhs=xq[a][0][:, cols].bitcast(FP8X4), rhs_scale=xq[a][1][:, cols], start=(a == 0), stop=(a == hb - 1),
                         )
             for d in range(cnt):
                 m = m0 + d
                 for a in range(hb):
                     nc.tensor.matmul_mx(
                         out=ya[:, d, :], lhsT=w2_codes[:, (m * hb + a) * P : (m * hb + a + 1) * P].bitcast(FP8X4), lhsT_scale=w2_scales[:, (m * hb + a) * P : (m * hb + a + 1) * P],
-                        rhs=xq[a][0][:, u * HALF : (u + 1) * HALF].bitcast(FP8X4), rhs_scale=xq[a][1][:, u * HALF : (u + 1) * HALF], start=(a == 0), stop=(a == hb - 1),
+                        rhs=xq[a][0][:, j0:j1].bitcast(FP8X4), rhs_scale=xq[a][1][:, j0:j1], start=(a == 0), stop=(a == hb - 1),
                     )
-            y = turn(ring, [P, cnt * HALF], F32, "raw" if u == 0 else "tab", 3)
-            nc.scalar.copy(y[:], ya[:].rearrange("p d c -> p (d c)"))
-            y3 = y[:].rearrange("p (d c) -> p d c", d=cnt)
-            nc.gpsimd.tensor_tensor(y3, y3, wgo_sb[:, u * HALF : (u + 1) * HALF].unsqueeze(1).to_broadcast([P, cnt, HALF]), MULT)
-            sq = ring.tile([P, cnt * HALF], F32, name="sq", tag="sq", bufs=1)
+            y = turn(ring, [P, cnt, width], F32, "raw" if m0 < 2 else "tab", 3)
+            nc.vector.tensor_tensor(y[:], ya[:], wgo_sb[:, j0:j1].unsqueeze(1).to_broadcast([P, cnt, width]), MULT)
+            sq = ring.tile([P, cnt * width], F32, name="sq", tag="sq", bufs=1)
             nc.scalar.activation(sq[:], yb[:].rearrange("p d c -> p (d c)"), ACT.Square)
-            rs = ring.tile([P, cnt * HALF], F32, name="rs", tag="rs", bufs=1)
+            rs = ring.tile([P, cnt * width], F32, name="rs", tag="rs", bufs=1)
             nc.scalar.activation(rs[:], sq[:], ACT.Abs_reciprocal_sqrt, bias=one[:])
-            damp = turn(ring, [P, cnt * HALF], F32, "gm_sb", 4)
+            damp = turn(ring, [P, cnt * width], F32, "gm_sb", 4)
             nc.scalar.activation(damp[:], rs[:], ACT.Square)
-            nc.gpsimd.tensor_tensor(y[:], y[:], damp[:], MULT)
             for d in range(cnt):
                 m = m0 + d
-                nc.vector.tensor_copy(cutter[m][:].indirect(idx4[:, u * LC : (u + 1) * LC]), y[:, d * HALF : (d + 1) * HALF])
-                if u == 1:
+                nc.vector.tensor_tensor(
+                    cutter[m][:].indirect(idx4[:, j0 // 16 : j1 // 16]), y[:, d, :], damp[:, d * width : (d + 1) * width], MULT
+                )
+                if j1 == R:
                     nc.sync.dma_start(out[m * P : (m + 1) * P, :], cutter[m][:])
 
-        unit(0, 0, 1)
-        unit(0, 1, 1)
+        unit(0, 1, 0, HALF)
+        unit(1, 1, 0, HALF)
         for i in range(PACK, 2 * PACK):
             scale_rows(i, picked[:, i - PACK, :], rows)
         quantize_x(rows, 1, HALF, R)
-        for u, m0, cnt in ((0, 2, 2), (0, 4, 2), (1, 0, 2), (1, 2, 2), (1, 4, 2)):
-            unit(u, m0, cnt)
+        unit(0, 2, HALF, R)
+        for m in range(2, nm):
+            unit(m, 1, 0, R)

from contextlib import ExitStack

import concourse.mybir as mybir

K, H, N, T, S, T2, R = 1536, 1024, 768, 2048, 512, 1024, 512
FLOPS = 2 * K * H * S + 2 * 2 * H * N * R

F32 = mybir.dt.float32
BF16 = mybir.dt.bfloat16
I32 = mybir.dt.int32
U32 = mybir.dt.uint32
U16 = mybir.dt.uint16
U8 = mybir.dt.uint8
FP8X4 = mybir.dt.float8_e4m3fn_x4
FP4X4 = mybir.dt.float4_e2m1fn_x4
MULT = mybir.AluOpType.mult
ACT = mybir.ActivationFunctionType

P = 128
PACK = 4
KP = P * PACK


def tile_list_hide_cutter_page_kernel(tc, tab_words, tab_scales, offs, w1, gm, wgs, page0, offs2, offs3, gain, w2, w4_words, w4_scales, wgo, page1, offs4, out):
    nc = tc.nc
    ka = K // KP
    hb = H // KP
    nm = N // P
    with ExitStack() as ctx:
        lists = ctx.enter_context(tc.tile_pool(name="lists", bufs=1))
        keep = ctx.enter_context(tc.tile_pool(name="keep", bufs=1))
        ring = ctx.enter_context(tc.tile_pool(name="ring", bufs=3))
        psum = ctx.enter_context(tc.psum_pool(name="psum", bufs=1))

        turns = {}

        def turn(pool, shape, dtype, tag, slots, align=None):
            k = turns.get(tag, 0)
            turns[tag] = k + 1
            return pool.tile(shape, dtype, name=tag, tag="%s%d" % (tag, k % slots), bufs=1, align_bytes=align)

        def load_list(src, name):
            t = lists.tile([P, src.shape[1]], U16, name=name)
            nc.sync.dma_start(t[:], src)
            return t

        idx = load_list(offs, "idx")
        tab_sc = keep.tile([P, T], U8, name="tab_sc")
        nc.gpsimd.memset(tab_sc[:].bitcast(I32), 0)
        w4_sc = keep.tile([P, hb * N], U8, name="w4_sc", align_bytes=64)
        nc.gpsimd.memset(w4_sc[:].bitcast(I32), 0)
        seed = keep.tile([P, 1], F32, name="seed")
        nc.gpsimd.memset(seed[:], 1.0)
        warm = keep.tile([P, 1], F32, name="warm")
        nc.scalar.activation(warm[:], seed[:], ACT.Abs_reciprocal_sqrt)
        one = keep.tile([P, 1], F32, name="one")
        nc.scalar.activation(one[:], warm[:], ACT.Copy, scale=0.0, bias=1.0)

        def load_rows(w, a, c0, c1, tag="raw", bufs=3):
            raw = turn(ring, [P, PACK, c1 - c0], F32, tag, bufs)
            nc.sync.dma_start(raw[:], w[a * KP : (a + 1) * KP, c0:c1].rearrange("(p j) c -> p j c", j=PACK))
            return raw

        def quantize(grouped, codes, scales):
            nc.vector.quantize_mx(out=codes.bitcast(FP8X4), scales=scales, in_=grouped)

        def w1_chunk(raw, a, b):
            grouped = turn(ring, [P, PACK * KP], BF16, "grouped", 3, 64)
            cast = nc.vector.tensor_copy if (a, b) == (1, 0) else nc.scalar.copy
            cast(
                grouped[:].rearrange("p (t m j) -> p m t j", t=PACK, j=PACK),
                raw[:].rearrange("p j (m t) -> p m t j", t=PACK),
            )
            codes = keep.tile([P, KP], U32, name="w1c%d%d" % (a, b), align_bytes=64)
            scales = keep.tile([P, KP], U8, name="w1s%d%d" % (a, b), align_bytes=64)
            quantize(grouped[:], codes[:], scales[:])
            return codes, scales

        w1q = {}
        v_codes = []

        def gather_pass(a):
            tab = turn(ring, [P, T], I32, "tab", 3)
            nc.sync.dma_start(tab[:], tab_words[a].rearrange("p t i -> p (t i)").bitcast(I32))
            vc = keep.tile([P, S], U32, name="vc%d" % a, align_bytes=64)
            nc.vector.tensor_copy(vc[:], tab[:].bitcast(U32).indirect(idx[:]))
            v_codes.append(vc)

        for a in range(2):
            w1q[a, 0] = w1_chunk(load_rows(w1, a, 0, KP), a, 0)
        for q in range(4):
            nc.sync.dma_start(tab_sc[32 * q : 32 * q + 4 * ka, :].bitcast(I32), tab_scales[:, 4 * q : 4 * q + 4, :].bitcast(I32))
        v_sc = keep.tile([P, S], U8, name="v_sc", align_bytes=64)
        nc.vector.tensor_copy(v_sc[:], tab_sc[:].indirect(idx[:]))
        gather_pass(0)
        w1q[2, 0] = w1_chunk(load_rows(w1, 2, 0, KP), 2, 0)
        gather_pass(1)
        gather_pass(2)

        def stage1(b):
            banks = [turn(psum, [P, S], F32, "acc", 8) for t in range(PACK)]
            for a in range(ka):
                codes, scales = w1q[a, b]
                for t in range(PACK):
                    cols = slice(t * P, (t + 1) * P)
                    nc.tensor.matmul_mx(
                        out=banks[t][:], lhsT=codes[:, cols].bitcast(FP8X4), lhsT_scale=scales[:, cols],
                        rhs=v_codes[a][:].bitcast(FP8X4), rhs_scale=v_sc[4 * a : P, :],
                        start=(a == 0), stop=(a == ka - 1),
                    )
            return banks

        gm_rows = gm.rearrange("(b p t) j -> b t p j", p=P, t=PACK)
        page0_rows = page0.rearrange("(b p t) j -> b t p j", p=P, t=PACK)
        wgs_rows = wgs.rearrange("(q t) j -> q t j", t=PACK)

        def load_gm(i):
            g = turn(ring, [P, S], F32, "gm_sb", 4)
            nc.sync.dma_start(g[:], gm_rows[i // PACK, i % PACK])
            return g

        def load_page0(i):
            pg = keep.tile([P, T2], F32, name="page0_%d" % i)
            nc.sync.dma_start(pg[:], page0_rows[i // PACK, i % PACK])
            return pg

        h_banks = stage1(0)
        gms = [load_gm(0)]
        wgs_sb = keep.tile([P, PACK, S], F32, name="wgs_sb", tag="late", align_bytes=64)
        for q in (0, 2, 1, 3):
            nc.sync.dma_start(wgs_sb[32 * q : 32 * q + 32, 0, :], wgs_rows[:, 0, :])
        idx2 = load_list(offs2, "idx2")
        idx3 = load_list(offs3, "idx3")
        pages = [load_page0(0)]
        gms.append(load_gm(1))
        for q in (0, 2, 1, 3):
            nc.sync.dma_start(wgs_sb[32 * q : 32 * q + 32, 1:PACK, :], wgs_rows[:, 1:PACK, :])
        pages.append(load_page0(1))
        gms.append(load_gm(2))
        raws = [load_rows(w1, 0, KP, 2 * KP)]
        pages.append(load_page0(2))
        gms.append(load_gm(3))
        raws.append(load_rows(w1, 1, KP, 2 * KP))
        raws.append(load_rows(w1, 2, KP, 2 * KP, "raw_last", 1))
        gain_sb = keep.tile([P, hb * PACK], F32, name="gain_sb")
        nc.sync.dma_start(gain_sb[:].rearrange("p (b t) -> p b t", b=hb), gain.rearrange("(b p t) -> p b t", b=hb, t=PACK))
        pages.append(load_page0(3))
        gms.append(load_gm(4))
        pages.append(load_page0(4))
        gms.append(load_gm(5))
        w2_cuts = ((0, KP), (KP, N))
        w2_raw = [[load_rows(w2, 0, c0, c1, "tab") for c0, c1 in w2_cuts]]
        pages.append(load_page0(5))
        gms.append(load_gm(6))
        w2_raw.append([load_rows(w2, 1, 0, KP, "tab"), load_rows(w2, 1, KP, N)])
        pages.append(load_page0(6))
        gms.append(load_gm(7))
        pages.append(load_page0(7))
        for q in range(4):
            nc.sync.dma_start(
                w4_sc[32 * q : 32 * q + 4, :].bitcast(I32).rearrange("r (a c) -> r a c", a=hb),
                w4_scales[:, 4 * q : 4 * q + 4, :].bitcast(I32).rearrange("a r c -> r a c"),
            )
        w4_sb = keep.tile([P, hb * 2 * N], U8, name="w4_sb", align_bytes=64)
        nc.sync.dma_start(w4_sb[:].bitcast(I32).rearrange("p (a c) -> p a c", a=hb), w4_words.bitcast(I32).rearrange("a p c -> p a c"))
        wgo_sb = keep.tile([P, R], F32, name="wgo_sb")
        nc.sync.dma_start(wgo_sb[:], wgo)
        idx4 = load_list(offs4, "idx4")
        cutter = []
        for m in range(nm):
            pg = keep.tile([P, T2], F32, name="page1_%d" % m)
            nc.sync.dma_start(pg[:], page1[m * P : (m + 1) * P, :])
            cutter.append(pg)

        HALF = R // 2
        hs = {}

        def make_h(i):
            hs[i] = turn(ring, [P, S], F32, "h", 3)
            nc.vector.tensor_tensor(hs[i][:], h_banks[i][:], gms[i][:], MULT)

        def put_h(i):
            nc.vector.tensor_tensor(pages[i][:].indirect(idx2[:]), hs[i][:], wgs_sb[:, i % PACK, :], MULT)

        def pick(i, c0, c1, dst):
            nc.vector.tensor_copy(dst, pages[i][:].indirect(idx3[:, c0 // 16 : c1 // 16]))

        def scale_rows(i, src, rows):
            nc.scalar.activation(rows[:, i % PACK, :], src, ACT.Copy, scale=gain_sb[:, i : i + 1])

        xq = [
            (keep.tile([P, R], U32, name="xc%d" % b, align_bytes=64), keep.tile([P, R], U8, name="xs%d" % b, align_bytes=64))
            for b in range(hb)
        ]

        def quantize_x(rows, b, c0, c1, tag="grouped", bufs=3):
            grouped = turn(ring, [P, PACK * (c1 - c0)], BF16, tag, bufs, 64)
            nc.scalar.copy(
                grouped[:].rearrange("p (c i t) -> p c t i", i=4, t=PACK),
                rows[:].rearrange("p t (c i) -> p c t i", i=4),
            )
            quantize(grouped[:], xq[b][0][:, c0:c1], xq[b][1][:, c0:c1])

        w2_grouped = keep.tile([P, hb * N * PACK], BF16, name="w2_grouped", align_bytes=64)

        def w2_cast(a):
            for (c0, c1), raw in zip(w2_cuts, w2_raw[a]):
                nc.scalar.copy(
                    w2_grouped[:].rearrange("p (m a c i j) -> p a m c j i", a=hb, c=P // 4, i=4, j=PACK)[:, a, c0 // P : c1 // P],
                    raw[:].rearrange("p j (m c i) -> p m c j i", c=P // 4, i=4),
                )

        picked = keep.tile([P, PACK, R], F32, name="picked")
        make_h(0)
        for i in range(PACK):
            put_h(i)
            if i < PACK - 1:
                make_h(i + 1)
                w1q[i, 1] = w1_chunk(raws[i], i, 1)
            pick(i, 0, R, picked[:, i, :])
        h_banks.extend(stage1(1))
        make_h(PACK)
        pass
        rows = turn(ring, [P, PACK, R], BF16, "raw_last", 1)
        for i in range(PACK):
            scale_rows(i, picked[:, i, :], rows)
        quantize_x(rows, 0, 0, R)
        picked = keep.tile([P, PACK, HALF], F32, name="picked_a")
        rows = keep.tile([P, PACK, HALF], BF16, name="rows_a")
        for i in range(PACK, 2 * PACK):
            put_h(i)
            if i < 2 * PACK - 1:
                make_h(i + 1)
            pick(i, 0, HALF, picked[:, i - PACK, :])
            scale_rows(i, picked[:, i - PACK, :], rows)
            if i - PACK < hb:
                w2_cast(i - PACK)
        quantize_x(rows, 1, 0, HALF, "late_codes", 1)
        pass
        w2_codes = turn(ring, [P, hb * N], U32, "late_codes", 1, 64)
        w2_scales = keep.tile([P, hb * N], U8, name="w2_scales", align_bytes=64)
        picked = keep.tile([P, PACK, HALF], F32, name="picked_b", tag="late", align_bytes=64)
        rows = keep.tile([P, PACK, HALF], BF16, name="rows_b")
        for i in range(PACK, 2 * PACK):
            pick(i, HALF, R, picked[:, i - PACK, :])
        for c0, c1 in ((0, 1024), (1024, hb * N)):
            quantize(w2_grouped[:, c0 * PACK : c1 * PACK], w2_codes[:, c0:c1], w2_scales[:, c0:c1])

        def unit(m0, cnt, j0, j1):
            width = j1 - j0
            yb = turn(psum, [P, cnt, width], F32, "acc", 8)
            ya = turn(psum, [P, cnt, width], F32, "acc", 8)
            step = R if width == R else P
            for d in range(cnt):
                m = m0 + d
                for c0 in range(0, width, step):
                    cols = slice(j0 + c0, j0 + c0 + step)
                    for a in range(hb):
                        nc.tensor.matmul_mx(
                            out=yb[:, d, c0 : c0 + step], lhsT=w4_sb[:, a * 2 * N + 2 * m * P : a * 2 * N + 2 * (m + 1) * P].bitcast(FP4X4),
                            lhsT_scale=w4_sc[:, a * N + m * P : a * N + (m + 1) * P],
                            rhs=xq[a][0][:, cols].bitcast(FP8X4), rhs_scale=xq[a][1][:, cols], start=(a == 0), stop=(a == hb - 1),
                        )
            for d in range(cnt):
                m = m0 + d
                for a in range(hb):
                    nc.tensor.matmul_mx(
                        out=ya[:, d, :], lhsT=w2_codes[:, (m * hb + a) * P : (m * hb + a + 1) * P].bitcast(FP8X4), lhsT_scale=w2_scales[:, (m * hb + a) * P : (m * hb + a + 1) * P],
                        rhs=xq[a][0][:, j0:j1].bitcast(FP8X4), rhs_scale=xq[a][1][:, j0:j1], start=(a == 0), stop=(a == hb - 1),
                    )
            y = turn(ring, [P, cnt, width], F32, "raw" if m0 < 2 else "tab", 3)
            nc.vector.tensor_tensor(y[:], ya[:], wgo_sb[:, j0:j1].unsqueeze(1).to_broadcast([P, cnt, width]), MULT)
            sq = ring.tile([P, cnt * width], F32, name="sq", tag="sq", bufs=1)
            nc.scalar.activation(sq[:], yb[:].rearrange("p d c -> p (d c)"), ACT.Square)
            rs = ring.tile([P, cnt * width], F32, name="rs", tag="rs", bufs=1)
            nc.scalar.activation(rs[:], sq[:], ACT.Abs_reciprocal_sqrt, bias=one[:])
            damp = turn(ring, [P, cnt * width], F32, "gm_sb", 4)
            nc.scalar.activation(damp[:], rs[:], ACT.Square)
            for d in range(cnt):
                m = m0 + d
                nc.vector.tensor_tensor(
                    cutter[m][:].indirect(idx4[:, j0 // 16 : j1 // 16]), y[:, d, :], damp[:, d * width : (d + 1) * width], MULT
                )
                if j1 == R:
                    nc.sync.dma_start(out[m * P : (m + 1) * P, :], cutter[m][:])

        unit(0, 1, 0, HALF)
        unit(1, 1, 0, HALF)
        for i in range(PACK, 2 * PACK):
            scale_rows(i, picked[:, i - PACK, :], rows)
        quantize_x(rows, 1, HALF, R)
        unit(0, 2, HALF, R)
        for m in range(2, nm):
            unit(m, 1, 0, R)
